import numpy as np
import ml_dtypes


def mxq(x, axis, fmt="e4m3"):
    dtype, down = {"e4m3": (ml_dtypes.float8_e4m3fn, 7), "e5m2": (ml_dtypes.float8_e5m2, 14)}[fmt]
    v = np.moveaxis(np.asarray(x, np.float32).astype(ml_dtypes.bfloat16).astype(np.float64), axis, -1)
    blocks = v.reshape(v.shape[:-1] + (-1, 32))
    amax = np.abs(blocks).max(-1, keepdims=True)
    byte = np.maximum(np.where(amax > 0, np.frexp(amax)[1] - 1 + 127, 0) - down, 1)
    scale = np.exp2(byte - 127.0)
    codes = (blocks / scale).astype(np.float32).astype(dtype).astype(np.float64)
    return np.moveaxis((codes * scale).reshape(v.shape), -1, axis)


WIDE = False


def mx_kscale(k):
    if not WIDE:
        return np.ones(k)
    levels = np.array([10, -10, 5, -5, 0])
    if k % 512:
        return np.exp2(np.random.permutation(np.resize(levels, k // 32))).repeat(32)
    a = np.empty((k // 512, 16))
    for p in range(k // 512):
        a[p, :8] = np.random.permutation(np.resize(levels, 8))
        for g in range(8):
            far = levels[np.abs(levels - a[p, g]) >= 10]
            a[p, g + 8] = far[np.random.randint(len(far))]
    return np.exp2(a.ravel()).repeat(32)


def f64(x):
    return np.asarray(x).astype(np.float64)


def striped(idx):
    return np.tile(np.asarray(idx).reshape(-1, 16).T, (8, 1)).astype(np.uint16)


def unstriped(offs):
    return offs[:16].T.reshape(-1).astype(np.int64)


E2M1 = np.array([0.0, 0.5, 1.0, 1.5, 2.0, 3.0, 4.0, 6.0, -0.0, -0.5, -1.0, -1.5, -2.0, -3.0, -4.0, -6.0])


def pack_weight(w, fmt):
    k, n = w.shape
    w = f64(np.asarray(w, np.float32).astype(ml_dtypes.bfloat16)).reshape(k // 32, 32, n)
    amax = np.abs(w).max(1)
    if fmt == "e4m3":
        byte = np.frexp(amax)[1] - 1 + 127 - 7
    else:
        mant, ex = np.frexp(amax / 6.0)
        byte = np.where(mant > 0.5, ex, ex - 1) + 127
    byte = np.clip(np.where(amax > 0, byte, 1), 1, 254)
    scaled = (w * np.exp2(127.0 - byte)[:, None, :]).reshape(k, n).astype(np.float32)
    by_word = np.ascontiguousarray(scaled.reshape(k // 512, 128, 4, n).transpose(0, 1, 3, 2))
    if fmt == "e4m3":
        words = by_word.astype(ml_dtypes.float8_e4m3fn).view(np.uint8)
    else:
        c = by_word.astype(ml_dtypes.float4_e2m1fn).view(np.uint8) & 0xF
        words = (c[..., 0::2] | (c[..., 1::2] << 4)).reshape(k // 512, 128, 2 * n)
    return np.ascontiguousarray(words), np.ascontiguousarray(byte.astype(np.uint8).reshape(k // 512, 16, n))


def unpack_weight(words, scales, fmt):
    g, _, n = scales.shape
    words = np.ascontiguousarray(words).reshape(g, 128, n, -1)
    if fmt == "e4m3":
        vals = words.view(ml_dtypes.float8_e4m3fn).astype(np.float64)
    else:
        nib = np.empty((g, 128, n, 4), np.uint8)
        nib[..., 0::2] = words & 0xF
        nib[..., 1::2] = words >> 4
        vals = E2M1[nib]
    vals = vals * np.repeat(np.exp2(scales.astype(np.float64) - 127.0), 8, axis=1)[..., None]
    return vals.transpose(0, 1, 3, 2).reshape(g * 512, n)


D, E, T, I, Q = 512, 512, 2048, 512, 128


def setup_inputs():
    n = np.random.standard_normal
    idx4 = np.random.permutation(I)[:I]
    idx = np.random.permutation(T)[:I]
    fd = mx_kscale(D)
    fe = mx_kscale(E)
    keysp = pack_weight(n((D, T)) / fd[:, None], "e4m3")
    valsp = pack_weight(n((E, T)) / fe[:, None], "e4m3")
    return {
        "query": (n((D, Q)) * 0.8 / np.sqrt(D) * fd[:, None]).astype(np.float32),
        "keys_words": keysp[0],
        "keys_scales": keysp[1],
        "pull": (np.random.uniform(0.4, 1.2, (Q, 1))).astype(np.float32),
        "gout": (n((E, Q)) * 1 / np.sqrt(E) * fe[:, None]).astype(np.float32),
        "vals_words": valsp[0],
        "vals_scales": valsp[1],
        "dquery": (n((D, Q)) * 1.0 / np.sqrt(D) * fd[:, None]).astype(np.float32),
        "base": (0.5 * n((Q, T))).astype(np.float32),
        "offs4": striped(idx4),
        "offs": striped(idx),
    }


def reference(query, keys_words, keys_scales, pull, gout, vals_words, vals_scales, dquery, base, offs4, offs):
    idx4 = unstriped(offs4)
    idx = unstriped(offs)
    keysu = unpack_weight(keys_words, keys_scales, "e4m3")
    valsu = unpack_weight(vals_words, vals_scales, "e4m3")
    queryq = mxq(f64(query), 0, "e4m3")
    keysidxg = keysu[:, idx]
    a = queryq.T @ keysidxg
    dqueryq = mxq(f64(dquery), 0, "e4m3")
    ta = dqueryq.T @ keysidxg
    p = np.exp(a - np.max(a, axis=1, keepdims=True))
    goutq = mxq(f64(gout), 0, "e4m3")
    valsidxg = valsu[:, idx]
    c0 = goutq.T @ valsidxg
    e1 = c0 * f64(pull)
    s1 = np.zeros((Q, I))
    s1[:, idx4] = e1
    dr = c0 + s1
    dp = dr / np.sum(p, axis=1, keepdims=True) + np.sum(dr * p / np.square(np.sum(p, axis=1, keepdims=True)) * (-1.0), axis=1, keepdims=True)
    tp = ta * p
    tdp = np.sum(tp, axis=1, keepdims=True) * dr / np.square(np.sum(p, axis=1, keepdims=True)) * (-1.0) + np.sum((tp * dr - np.sum(tp, axis=1, keepdims=True) * np.sum(p, axis=1, keepdims=True) * 2.0 * dr * p / np.square(np.sum(p, axis=1, keepdims=True))) / np.square(np.sum(p, axis=1, keepdims=True)) * (-1.0), axis=1, keepdims=True)
    tda = tdp * p + tp * dp
    gs = tda * 512.0
    gf = np.zeros((Q, T))
    gf[:, idx] = gs
    y = f64(base) + gf
    return y

@@ -1,0 +1,172 @@
+from contextlib import ExitStack
+
+import concourse.mybir as mybir
+
+F32 = mybir.dt.float32
+BF16 = mybir.dt.bfloat16
+I32 = mybir.dt.int32
+U32 = mybir.dt.uint32
+U16 = mybir.dt.uint16
+U8 = mybir.dt.uint8
+FP8X4 = mybir.dt.float8_e4m3fn_x4
+ALU = mybir.AluOpType
+ACT = mybir.ActivationFunctionType
+
+P = 128
+PACK = 4
+TOKENS = 2048
+SLOTS = 512
+ROWS = 128
+HALF = SLOTS // 2
+LIST_COLS = SLOTS // 16
+STORE_WIDTHS = (256, 512, 512, 512, 256)
+
+FLOPS = 3 * 2 * 512 * ROWS * SLOTS
+
+
+def tile_attend_hvdirect_followed_s_kernel(
+    tc, query, keys_words, keys_scales, pull, gout, vals_words, vals_scales, dquery, base, offs4, offs, out
+):
+    nc = tc.nc
+    with ExitStack() as ctx:
+        lists = ctx.enter_context(tc.tile_pool(name="lists", bufs=1))
+        sb = ctx.enter_context(tc.tile_pool(name="sb", bufs=1))
+        shared = ctx.enter_context(tc.tile_pool(name="shared", bufs=1))
+        psum = ctx.enter_context(tc.psum_pool(name="psum", bufs=1))
+
+        def load_rows(raw, src):
+            nc.sync.dma_start(out=raw[:], in_=src.rearrange("(p j) q -> p j q", j=PACK))
+
+        def quantise(raw, name, tag):
+            grouped = sb.tile([P, ROWS, PACK], BF16, name=name + "_grouped", tag=tag, align_bytes=64)
+            nc.vector.tensor_copy(out=grouped[:], in_=raw[:].rearrange("p j q -> p q j"))
+            codes = sb.tile([P, ROWS], U32, name=name + "_codes", align_bytes=64)
+            scales = sb.tile([P, ROWS], U8, name=name + "_scales", align_bytes=64)
+            nc.vector.quantize_mx(
+                out=codes[:].bitcast(FP8X4), scales=scales[:], in_=grouped[:].rearrange("p q j -> p (q j)")
+            )
+            return codes, scales
+
+        def load_scale_rows(queue, plane, src):
+            rows = src[0].bitcast(I32)
+            for r in range(4):
+                queue.dma_start(out=plane[r:P:32, :].bitcast(I32), in_=rows[r:16:4, :])
+
+        def load_words(window, src):
+            nc.sync.dma_start(
+                out=window[:].bitcast(I32), in_=src[0].rearrange("p n t -> p (n t)").bitcast(I32)
+            )
+
+        def product(bank, cols, codes, scales, words, word_scales):
+            nc.tensor.matmul_mx(
+                out=bank[:, cols],
+                lhsT=codes[:].bitcast(FP8X4),
+                lhsT_scale=scales[:],
+                rhs=words[:, cols].bitcast(FP8X4),
+                rhs_scale=word_scales[:, cols],
+                start=True,
+                stop=True,
+            )
+
+        halves = [(slice(h * HALF, (h + 1) * HALF), slice(h * LIST_COLS // 2, (h + 1) * LIST_COLS // 2)) for h in range(2)]
+
+        vs_win = sb.tile([P, TOKENS], U8, name="vs_win", tag="vs_then_vw", align_bytes=64)
+        ks_win = sb.tile([P, TOKENS], U8, name="ks_win", tag="ks_then_kw", align_bytes=64)
+        nc.vector.memset(vs_win[:].bitcast(I32), 0)
+        nc.vector.memset(ks_win[:].bitcast(I32), 0)
+
+        idx = lists.tile([P, LIST_COLS], U16, name="idx")
+        idx4 = lists.tile([P, LIST_COLS], U16, name="idx4")
+        nc.sync.dma_start(idx[:], offs)
+        gout_raw = shared.tile([P, PACK, ROWS], F32, name="gout_raw", offset=7168)
+        load_rows(gout_raw, gout)
+        vw_win = sb.tile([P, TOKENS], U32, name="vw_win", tag="vw_then_base")
+        load_words(vw_win, vals_words)
+        nc.sync.dma_start(idx4[:], offs4)
+        load_scale_rows(nc.scalar, vs_win, vals_scales)
+        pull_col = sb.tile([P, 1], F32, name="pull_col")
+        nc.gpsimd.dma_start(out=pull_col[:], in_=pull)
+        load_scale_rows(nc.gpsimd, ks_win, keys_scales)
+
+        g_codes, g_scales = quantise(gout_raw, "gout", "gout_then_dquery")
+        query_raw = shared.tile([P, PACK, ROWS], F32, name="query_raw", offset=8192)
+        load_rows(query_raw, query)
+        kw_win = shared.tile([P, TOKENS], U32, name="kw_win", offset=0)
+        load_words(kw_win, keys_words)
+
+        vs = sb.tile([P, SLOTS], U8, name="vs", align_bytes=64)
+        nc.vector.tensor_copy(vs[:], vs_win[:].indirect(idx[:]))
+        dquery_raw = sb.tile([P, PACK, ROWS], F32, name="dquery_raw", tag="gout_then_dquery", align_bytes=64)
+        load_rows(dquery_raw, dquery)
+
+        vw = sb.tile([P, SLOTS], U32, name="vw", tag="vs_then_vw", align_bytes=64)
+        c0 = psum.tile([P, SLOTS], F32, name="c0")
+        e1 = sb.tile([P, SLOTS], F32, name="e1")
+        s1 = sb.tile([P, SLOTS], F32, name="s1")
+        for cols, entries in halves:
+            nc.vector.tensor_copy(vw[:, cols], vw_win[:].indirect(idx[:, entries]))
+            product(c0, cols, g_codes, g_scales, vw, vs)
+            nc.scalar.activation(e1[:, cols], c0[:, cols], ACT.Copy, scale=pull_col[:])
+            nc.scalar.activation(s1[:].indirect(idx4[:, entries]), e1[:, cols], ACT.Copy)
+
+        base_sb = sb.tile([P, TOKENS], F32, name="base_sb", tag="vw_then_base")
+        nc.sync.dma_start(out=base_sb[:], in_=base)
+
+        ks = sb.tile([P, SLOTS], U8, name="ks", align_bytes=64)
+        nc.vector.tensor_copy(ks[:], ks_win[:].indirect(idx[:]))
+        q_codes, q_scales = quantise(query_raw, "query", "query_grouped")
+        kw = sb.tile([P, SLOTS], U32, name="kw", tag="ks_then_kw", align_bytes=64)
+        a = psum.tile([P, SLOTS], F32, name="a")
+        for cols, entries in halves:
+            nc.vector.tensor_copy(kw[:, cols], kw_win[:].indirect(idx[:, entries]))
+            product(a, cols, q_codes, q_scales, kw, ks)
+        dq_codes, dq_scales = quantise(dquery_raw, "dquery", "dquery_then_gf")
+        gf = sb.tile([P, TOKENS], F32, name="gf", tag="dquery_then_gf", align_bytes=64)
+        nc.gpsimd.memset(gf[:], 0.0)
+        ta = psum.tile([P, SLOTS], F32, name="ta")
+        product(ta, slice(0, SLOTS), dq_codes, dq_scales, kw, ks)
+
+        def column(name):
+            return sb.tile([P, 1], F32, name=name)
+
+        def wide(name):
+            return sb.tile([P, SLOTS], F32, name=name)
+
+        neg_max = column("neg_max")
+        nc.vector.tensor_reduce(out=neg_max[:], in_=a[:], axis=mybir.AxisListType.X, op=ALU.max, negate=True)
+        p = wide("p")
+        p_sum = column("p_sum")
+        nc.scalar.activation(p[:], a[:], ACT.Exp, bias=neg_max[:], accum_out=p_sum[:])
+        dr = wide("dr")
+        nc.vector.tensor_tensor(dr[:], c0[:], s1[:], ALU.add)
+
+        inv_sum = column("inv_sum")
+        nc.vector.reciprocal(inv_sum[:], p_sum[:])
+        neg_tp = wide("neg_tp")
+        neg_tp_sum = column("neg_tp_sum")
+        nc.vector.scalar_tensor_tensor(neg_tp[:], ta[:], -1.0, p[:], ALU.mult, ALU.mult, accum_out=neg_tp_sum[:])
+        gain = column("gain")
+        nc.vector.tensor_scalar(gain[:], inv_sum[:], inv_sum[:], 512.0, ALU.mult, ALU.mult)
+        ta_dev = wide("ta_dev")
+        nc.scalar.activation(ta_dev[:], ta[:], ACT.Identity, bias=neg_tp_sum[:], scale=p_sum[:])
+        dr_terms = wide("dr_terms")
+        dr_mean = column("dr_mean")
+        nc.vector.scalar_tensor_tensor(dr_terms[:], dr[:], inv_sum[:], p[:], ALU.mult, ALU.mult, accum_out=dr_mean[:])
+        tpdr_terms = wide("tpdr_terms")
+        tpdr_sum = column("tpdr_sum")
+        nc.vector.scalar_tensor_tensor(tpdr_terms[:], neg_tp[:], -1.0, dr[:], ALU.mult, ALU.mult, accum_out=tpdr_sum[:])
+        cov = column("cov")
+        nc.scalar.activation(cov[:], dr_mean[:], ACT.Identity, bias=tpdr_sum[:], scale=neg_tp_sum[:])
+        cross = wide("cross")
+        nc.vector.scalar_tensor_tensor(cross[:], dr[:], dr_mean[:], ta_dev[:], ALU.subtract, ALU.mult)
+        factor = wide("factor")
+        nc.vector.tensor_scalar(factor[:], cross[:], cov[:], gain[:], ALU.subtract, ALU.mult)
+        nc.vector.tensor_tensor(gf[:].indirect(idx[:]), factor[:], p[:], ALU.mult)
+
+        start = 0
+        for n, width in enumerate(STORE_WIDTHS):
+            cols = slice(start, start + width)
+            result = sb.tile([P, width], F32, name="result%d" % n)
+            nc.vector.tensor_tensor(result[:], base_sb[:, cols], gf[:, cols], ALU.add)
+            nc.sync.dma_start(out=out[:, cols], in_=result[:])
+            start += width

@@ -31,15 +31,17 @@ def tile_attend_hvdirect_followed_s_kernel(
     with ExitStack() as ctx:
         lists = ctx.enter_context(tc.tile_pool(name="lists", bufs=1))
         sb = ctx.enter_context(tc.tile_pool(name="sb", bufs=1))
-        shared = ctx.enter_context(tc.tile_pool(name="shared", bufs=1))
         psum = ctx.enter_context(tc.psum_pool(name="psum", bufs=1))
 
         def load_rows(raw, src):
             nc.sync.dma_start(out=raw[:], in_=src.rearrange("(p j) q -> p j q", j=PACK))
 
-        def quantise(raw, name, tag):
+        def quantise(raw, name, tag, on_scalar):
             grouped = sb.tile([P, ROWS, PACK], BF16, name=name + "_grouped", tag=tag, align_bytes=64)
-            nc.vector.tensor_copy(out=grouped[:], in_=raw[:].rearrange("p j q -> p q j"))
+            if on_scalar:
+                nc.scalar.activation(grouped[:], raw[:].rearrange("p j q -> p q j"), ACT.Copy)
+            else:
+                nc.vector.tensor_copy(out=grouped[:], in_=raw[:].rearrange("p j q -> p q j"))
             codes = sb.tile([P, ROWS], U32, name=name + "_codes", align_bytes=64)
             scales = sb.tile([P, ROWS], U8, name=name + "_scales", align_bytes=64)
             nc.vector.quantize_mx(
@@ -47,10 +49,10 @@ def tile_attend_hvdirect_followed_s_kernel(
             )
             return codes, scales
 
-        def load_scale_rows(queue, plane, src):
+        def load_scale_rows(plane, src):
             rows = src[0].bitcast(I32)
             for r in range(4):
-                queue.dma_start(out=plane[r:P:32, :].bitcast(I32), in_=rows[r:16:4, :])
+                nc.sync.dma_start(out=plane[r:P:32, :].bitcast(I32), in_=rows[r:16:4, :])
 
         def load_words(window, src):
             nc.sync.dma_start(
@@ -70,59 +72,66 @@ def tile_attend_hvdirect_followed_s_kernel(
 
         halves = [(slice(h * HALF, (h + 1) * HALF), slice(h * LIST_COLS // 2, (h + 1) * LIST_COLS // 2)) for h in range(2)]
 
-        vs_win = sb.tile([P, TOKENS], U8, name="vs_win", tag="vs_then_vw", align_bytes=64)
-        ks_win = sb.tile([P, TOKENS], U8, name="ks_win", tag="ks_then_kw", align_bytes=64)
+        vs_win = sb.tile([P, TOKENS], U8, name="vs_win")
+        ks_win = sb.tile([P, TOKENS], U8, name="ks_win")
+        gf = sb.tile([P, TOKENS], F32, name="gf")
         nc.vector.memset(vs_win[:].bitcast(I32), 0)
         nc.vector.memset(ks_win[:].bitcast(I32), 0)
+        nc.vector.memset(gf[:], 0.0)
 
         idx = lists.tile([P, LIST_COLS], U16, name="idx")
         idx4 = lists.tile([P, LIST_COLS], U16, name="idx4")
-        nc.sync.dma_start(idx[:], offs)
-        gout_raw = shared.tile([P, PACK, ROWS], F32, name="gout_raw", offset=7168)
-        load_rows(gout_raw, gout)
-        vw_win = sb.tile([P, TOKENS], U32, name="vw_win", tag="vw_then_base")
-        load_words(vw_win, vals_words)
-        nc.sync.dma_start(idx4[:], offs4)
-        load_scale_rows(nc.scalar, vs_win, vals_scales)
         pull_col = sb.tile([P, 1], F32, name="pull_col")
         nc.gpsimd.dma_start(out=pull_col[:], in_=pull)
-        load_scale_rows(nc.gpsimd, ks_win, keys_scales)
-
-        g_codes, g_scales = quantise(gout_raw, "gout", "gout_then_dquery")
-        query_raw = shared.tile([P, PACK, ROWS], F32, name="query_raw", offset=8192)
+        gout_raw = sb.tile([P, PACK, ROWS], F32, name="gout_raw", tag="gout_then_kw")
+        load_rows(gout_raw, gout)
+        vs_rows = sb.tile([P, TOKENS], U8, name="vs_rows")
+        load_scale_rows(vs_rows, vals_scales)
+        nc.sync.dma_start(idx[:], offs)
+        vw_win = sb.tile([P, TOKENS], U32, name="vw_win", tag="vw_then_base")
+        load_words(vw_win, vals_words)
+        query_raw = sb.tile([P, PACK, ROWS], F32, name="query_raw")
         load_rows(query_raw, query)
-        kw_win = shared.tile([P, TOKENS], U32, name="kw_win", offset=0)
-        load_words(kw_win, keys_words)
+        nc.sync.dma_start(idx4[:], offs4)
+        load_scale_rows(ks_win, keys_scales)
 
-        vs = sb.tile([P, SLOTS], U8, name="vs", align_bytes=64)
-        nc.vector.tensor_copy(vs[:], vs_win[:].indirect(idx[:]))
-        dquery_raw = sb.tile([P, PACK, ROWS], F32, name="dquery_raw", tag="gout_then_dquery", align_bytes=64)
+        g_codes, g_scales = quantise(gout_raw, "gout", "grouped_then_dquery", True)
+        kw_win = sb.tile([P, TOKENS], U32, name="kw_win", tag="gout_then_kw")
+        load_words(kw_win, keys_words)
+        dquery_raw = sb.tile([P, PACK, ROWS], F32, name="dquery_raw", tag="grouped_then_dquery", align_bytes=64)
         load_rows(dquery_raw, dquery)
 
-        vw = sb.tile([P, SLOTS], U32, name="vw", tag="vs_then_vw", align_bytes=64)
+        for quadrant in range(4):
+            live = slice(32 * quadrant, 32 * quadrant + 4)
+            nc.vector.tensor_copy(vs_win[live, :].bitcast(I32), vs_rows[live, :].bitcast(I32))
+        vs = sb.tile([P, SLOTS], U8, name="vs", align_bytes=64)
+        nc.vector.tensor_copy(vs[:], vs_win[:].indirect(idx[:]))
+
+        vw = sb.tile([P, SLOTS], U32, name="vw", align_bytes=64)
         c0 = psum.tile([P, SLOTS], F32, name="c0")
         e1 = sb.tile([P, SLOTS], F32, name="e1")
         s1 = sb.tile([P, SLOTS], F32, name="s1")
-        for cols, entries in halves:
+        for first, widths in ((0, (128,)), (128, (256, 128))):
+            cols = slice(first, first + sum(widths))
+            entries = slice(cols.start // 16, cols.stop // 16)
             nc.vector.tensor_copy(vw[:, cols], vw_win[:].indirect(idx[:, entries]))
-            product(c0, cols, g_codes, g_scales, vw, vs)
+            for width in widths:
+                product(c0, slice(first, first + width), g_codes, g_scales, vw, vs)
+                first += width
             nc.scalar.activation(e1[:, cols], c0[:, cols], ACT.Copy, scale=pull_col[:])
             nc.scalar.activation(s1[:].indirect(idx4[:, entries]), e1[:, cols], ACT.Copy)
-
         base_sb = sb.tile([P, TOKENS], F32, name="base_sb", tag="vw_then_base")
         nc.sync.dma_start(out=base_sb[:], in_=base)
 
+        q_codes, q_scales = quantise(query_raw, "query", "query_grouped", True)
         ks = sb.tile([P, SLOTS], U8, name="ks", align_bytes=64)
         nc.vector.tensor_copy(ks[:], ks_win[:].indirect(idx[:]))
-        q_codes, q_scales = quantise(query_raw, "query", "query_grouped")
-        kw = sb.tile([P, SLOTS], U32, name="kw", tag="ks_then_kw", align_bytes=64)
+        kw = sb.tile([P, SLOTS], U32, name="kw", align_bytes=64)
         a = psum.tile([P, SLOTS], F32, name="a")
         for cols, entries in halves:
             nc.vector.tensor_copy(kw[:, cols], kw_win[:].indirect(idx[:, entries]))
             product(a, cols, q_codes, q_scales, kw, ks)
-        dq_codes, dq_scales = quantise(dquery_raw, "dquery", "dquery_then_gf")
-        gf = sb.tile([P, TOKENS], F32, name="gf", tag="dquery_then_gf", align_bytes=64)
-        nc.gpsimd.memset(gf[:], 0.0)
+        dq_codes, dq_scales = quantise(dquery_raw, "dquery", "grouped_then_dr", False)
         ta = psum.tile([P, SLOTS], F32, name="ta")
         product(ta, slice(0, SLOTS), dq_codes, dq_scales, kw, ks)
 
@@ -132,12 +141,12 @@ def tile_attend_hvdirect_followed_s_kernel(
         def wide(name):
             return sb.tile([P, SLOTS], F32, name=name)
 
-        neg_max = column("neg_max")
+        neg_max = sb.tile([P, 1], F32, name="neg_max", tag="grouped_then_dquery", align_bytes=64)
         nc.vector.tensor_reduce(out=neg_max[:], in_=a[:], axis=mybir.AxisListType.X, op=ALU.max, negate=True)
         p = wide("p")
         p_sum = column("p_sum")
         nc.scalar.activation(p[:], a[:], ACT.Exp, bias=neg_max[:], accum_out=p_sum[:])
-        dr = wide("dr")
+        dr = sb.tile([P, SLOTS], F32, name="dr", tag="grouped_then_dr", align_bytes=64)
         nc.vector.tensor_tensor(dr[:], c0[:], s1[:], ALU.add)
 
         inv_sum = column("inv_sum")
@@ -158,9 +167,11 @@ def tile_attend_hvdirect_followed_s_kernel(
         cov = column("cov")
         nc.scalar.activation(cov[:], dr_mean[:], ACT.Identity, bias=tpdr_sum[:], scale=neg_tp_sum[:])
         cross = wide("cross")
-        nc.vector.scalar_tensor_tensor(cross[:], dr[:], dr_mean[:], ta_dev[:], ALU.subtract, ALU.mult)
         factor = wide("factor")
-        nc.vector.tensor_scalar(factor[:], cross[:], cov[:], gain[:], ALU.subtract, ALU.mult)
+        for cols, entries in halves:
+            nc.vector.scalar_tensor_tensor(cross[:, cols], dr[:, cols], dr_mean[:], ta_dev[:, cols], ALU.subtract, ALU.mult)
+        for cols, entries in halves:
+            nc.vector.tensor_scalar(factor[:, cols], cross[:, cols], cov[:], gain[:], ALU.subtract, ALU.mult)
         nc.vector.tensor_tensor(gf[:].indirect(idx[:]), factor[:], p[:], ALU.mult)
 
         start = 0

@@ -77,26 +77,27 @@ def tile_attend_hvdirect_followed_s_kernel(
         gf = sb.tile([P, TOKENS], F32, name="gf")
         nc.vector.memset(vs_win[:].bitcast(I32), 0)
         nc.vector.memset(ks_win[:].bitcast(I32), 0)
-        nc.vector.memset(gf[:], 0.0)
+        nc.vector.memset(gf[:].bitcast(I32), 0)
 
         idx = lists.tile([P, LIST_COLS], U16, name="idx")
         idx4 = lists.tile([P, LIST_COLS], U16, name="idx4")
         pull_col = sb.tile([P, 1], F32, name="pull_col")
-        nc.gpsimd.dma_start(out=pull_col[:], in_=pull)
-        gout_raw = sb.tile([P, PACK, ROWS], F32, name="gout_raw", tag="gout_then_kw")
+        gout_raw = sb.tile([P, PACK, ROWS], F32, name="gout_raw")
         load_rows(gout_raw, gout)
         vs_rows = sb.tile([P, TOKENS], U8, name="vs_rows")
         load_scale_rows(vs_rows, vals_scales)
         nc.sync.dma_start(idx[:], offs)
-        vw_win = sb.tile([P, TOKENS], U32, name="vw_win", tag="vw_then_base")
-        load_words(vw_win, vals_words)
         query_raw = sb.tile([P, PACK, ROWS], F32, name="query_raw")
         load_rows(query_raw, query)
+        vw_win = sb.tile([P, TOKENS], U32, name="vw_win", tag="vw_then_base")
+        load_words(vw_win, vals_words)
         nc.sync.dma_start(idx4[:], offs4)
+        nc.sync.dma_start(out=pull_col[:], in_=pull)
         load_scale_rows(ks_win, keys_scales)
 
         g_codes, g_scales = quantise(gout_raw, "gout", "grouped_then_dquery", True)
-        kw_win = sb.tile([P, TOKENS], U32, name="kw_win", tag="gout_then_kw")
+        q_codes, q_scales = quantise(query_raw, "query", "query_grouped", True)
+        kw_win = sb.tile([P, TOKENS], U32, name="kw_win")
         load_words(kw_win, keys_words)
         dquery_raw = sb.tile([P, PACK, ROWS], F32, name="dquery_raw", tag="grouped_then_dquery", align_bytes=64)
         load_rows(dquery_raw, dquery)
@@ -123,7 +124,6 @@ def tile_attend_hvdirect_followed_s_kernel(
         base_sb = sb.tile([P, TOKENS], F32, name="base_sb", tag="vw_then_base")
         nc.sync.dma_start(out=base_sb[:], in_=base)
 
-        q_codes, q_scales = quantise(query_raw, "query", "query_grouped", True)
         ks = sb.tile([P, SLOTS], U8, name="ks", align_bytes=64)
         nc.vector.tensor_copy(ks[:], ks_win[:].indirect(idx[:]))
         kw = sb.tile([P, SLOTS], U32, name="kw", align_bytes=64)
@@ -165,11 +165,12 @@ def tile_attend_hvdirect_followed_s_kernel(
         tpdr_sum = column("tpdr_sum")
         nc.vector.scalar_tensor_tensor(tpdr_terms[:], neg_tp[:], -1.0, dr[:], ALU.mult, ALU.mult, accum_out=tpdr_sum[:])
         cov = column("cov")
-        nc.scalar.activation(cov[:], dr_mean[:], ACT.Identity, bias=tpdr_sum[:], scale=neg_tp_sum[:])
         cross = wide("cross")
         factor = wide("factor")
         for cols, entries in halves:
             nc.vector.scalar_tensor_tensor(cross[:, cols], dr[:, cols], dr_mean[:], ta_dev[:, cols], ALU.subtract, ALU.mult)
+            if cols.start == 0:
+                nc.vector.tensor_scalar(cov[:], dr_mean[:], neg_tp_sum[:], tpdr_sum[:], ALU.mult, ALU.add)
         for cols, entries in halves:
             nc.vector.tensor_scalar(factor[:, cols], cross[:, cols], cov[:], gain[:], ALU.subtract, ALU.mult)
         nc.vector.tensor_tensor(gf[:].indirect(idx[:]), factor[:], p[:], ALU.mult)

@@ -82,21 +82,20 @@ def tile_attend_hvdirect_followed_s_kernel(
         idx = lists.tile([P, LIST_COLS], U16, name="idx")
         idx4 = lists.tile([P, LIST_COLS], U16, name="idx4")
         pull_col = sb.tile([P, 1], F32, name="pull_col")
-        gout_raw = sb.tile([P, PACK, ROWS], F32, name="gout_raw")
-        load_rows(gout_raw, gout)
+        nc.scalar.dma_start(out=pull_col[:], in_=pull)
         vs_rows = sb.tile([P, TOKENS], U8, name="vs_rows")
         load_scale_rows(vs_rows, vals_scales)
         nc.sync.dma_start(idx[:], offs)
-        query_raw = sb.tile([P, PACK, ROWS], F32, name="query_raw")
-        load_rows(query_raw, query)
+        gout_raw = sb.tile([P, PACK, ROWS], F32, name="gout_raw")
+        load_rows(gout_raw, gout)
         vw_win = sb.tile([P, TOKENS], U32, name="vw_win", tag="vw_then_base")
         load_words(vw_win, vals_words)
+        query_raw = sb.tile([P, PACK, ROWS], F32, name="query_raw", tag="query_then_e1")
+        load_rows(query_raw, query)
         nc.sync.dma_start(idx4[:], offs4)
-        nc.sync.dma_start(out=pull_col[:], in_=pull)
         load_scale_rows(ks_win, keys_scales)
 
         g_codes, g_scales = quantise(gout_raw, "gout", "grouped_then_dquery", True)
-        q_codes, q_scales = quantise(query_raw, "query", "query_grouped", True)
         kw_win = sb.tile([P, TOKENS], U32, name="kw_win")
         load_words(kw_win, keys_words)
         dquery_raw = sb.tile([P, PACK, ROWS], F32, name="dquery_raw", tag="grouped_then_dquery", align_bytes=64)
@@ -108,9 +107,10 @@ def tile_attend_hvdirect_followed_s_kernel(
         vs = sb.tile([P, SLOTS], U8, name="vs", align_bytes=64)
         nc.vector.tensor_copy(vs[:], vs_win[:].indirect(idx[:]))
 
+        q_codes, q_scales = quantise(query_raw, "query", "query_grouped", True)
         vw = sb.tile([P, SLOTS], U32, name="vw", align_bytes=64)
         c0 = psum.tile([P, SLOTS], F32, name="c0")
-        e1 = sb.tile([P, SLOTS], F32, name="e1")
+        e1 = sb.tile([P, SLOTS], F32, name="e1", tag="query_then_e1")
         s1 = sb.tile([P, SLOTS], F32, name="s1")
         for first, widths in ((0, (128,)), (128, (256, 128))):
             cols = slice(first, first + sum(widths))

@@ -38,10 +38,12 @@ def tile_attend_hvdirect_followed_s_kernel(
 
         def quantise(raw, name, tag, on_scalar):
             grouped = sb.tile([P, ROWS, PACK], BF16, name=name + "_grouped", tag=tag, align_bytes=64)
+            src = raw[:].rearrange("p j (c i) -> p c j i", i=4)
+            dst = grouped[:].rearrange("p (c i) j -> p c j i", i=4)
             if on_scalar:
-                nc.scalar.activation(grouped[:], raw[:].rearrange("p j q -> p q j"), ACT.Copy)
+                nc.scalar.activation(dst, src, ACT.Copy)
             else:
-                nc.vector.tensor_copy(out=grouped[:], in_=raw[:].rearrange("p j q -> p q j"))
+                nc.vector.tensor_copy(out=dst, in_=src)
             codes = sb.tile([P, ROWS], U32, name=name + "_codes", align_bytes=64)
             scales = sb.tile([P, ROWS], U8, name=name + "_scales", align_bytes=64)
             nc.vector.quantize_mx(
@@ -128,9 +130,13 @@ def tile_attend_hvdirect_followed_s_kernel(
         nc.vector.tensor_copy(ks[:], ks_win[:].indirect(idx[:]))
         kw = sb.tile([P, SLOTS], U32, name="kw", align_bytes=64)
         a = psum.tile([P, SLOTS], F32, name="a")
-        for cols, entries in halves:
+        for first, widths in ((0, (256, 128)), (384, (128,))):
+            cols = slice(first, first + sum(widths))
+            entries = slice(cols.start // 16, cols.stop // 16)
             nc.vector.tensor_copy(kw[:, cols], kw_win[:].indirect(idx[:, entries]))
-            product(a, cols, q_codes, q_scales, kw, ks)
+            for width in widths:
+                product(a, slice(first, first + width), q_codes, q_scales, kw, ks)
+                first += width
         dq_codes, dq_scales = quantise(dquery_raw, "dquery", "grouped_then_dr", False)
         ta = psum.tile([P, SLOTS], F32, name="ta")
         product(ta, slice(0, SLOTS), dq_codes, dq_scales, kw, ks)

from contextlib import ExitStack

import concourse.mybir as mybir

F32 = mybir.dt.float32
BF16 = mybir.dt.bfloat16
I32 = mybir.dt.int32
U32 = mybir.dt.uint32
U16 = mybir.dt.uint16
U8 = mybir.dt.uint8
FP8X4 = mybir.dt.float8_e4m3fn_x4
ALU = mybir.AluOpType
ACT = mybir.ActivationFunctionType

P = 128
PACK = 4
TOKENS = 2048
SLOTS = 512
ROWS = 128
HALF = SLOTS // 2
LIST_COLS = SLOTS // 16
STORE_WIDTHS = (256, 512, 512, 512, 256)

FLOPS = 3 * 2 * 512 * ROWS * SLOTS


def tile_attend_hvdirect_followed_s_kernel(
    tc, query, keys_words, keys_scales, pull, gout, vals_words, vals_scales, dquery, base, offs4, offs, out
):
    nc = tc.nc
    with ExitStack() as ctx:
        lists = ctx.enter_context(tc.tile_pool(name="lists", bufs=1))
        sb = ctx.enter_context(tc.tile_pool(name="sb", bufs=1))
        psum = ctx.enter_context(tc.psum_pool(name="psum", bufs=1))

        def load_rows(raw, src):
            nc.sync.dma_start(out=raw[:], in_=src.rearrange("(p j) q -> p j q", j=PACK))

        def quantise(raw, name, tag, on_scalar):
            grouped = sb.tile([P, ROWS, PACK], BF16, name=name + "_grouped", tag=tag, align_bytes=64)
            src = raw[:].rearrange("p j (c i) -> p c j i", i=4)
            dst = grouped[:].rearrange("p (c i) j -> p c j i", i=4)
            if on_scalar:
                nc.scalar.activation(dst, src, ACT.Copy)
            else:
                nc.vector.tensor_copy(out=dst, in_=src)
            codes = sb.tile([P, ROWS], U32, name=name + "_codes", align_bytes=64)
            scales = sb.tile([P, ROWS], U8, name=name + "_scales", align_bytes=64)
            nc.vector.quantize_mx(
                out=codes[:].bitcast(FP8X4), scales=scales[:], in_=grouped[:].rearrange("p q j -> p (q j)")
            )
            return codes, scales

        def load_scale_rows(plane, src):
            rows = src[0].bitcast(I32)
            for r in range(4):
                nc.sync.dma_start(out=plane[r:P:32, :].bitcast(I32), in_=rows[r:16:4, :])

        def load_words(window, src):
            nc.sync.dma_start(
                out=window[:].bitcast(I32), in_=src[0].rearrange("p n t -> p (n t)").bitcast(I32)
            )

        def product(bank, cols, codes, scales, words, word_scales):
            nc.tensor.matmul_mx(
                out=bank[:, cols],
                lhsT=codes[:].bitcast(FP8X4),
                lhsT_scale=scales[:],
                rhs=words[:, cols].bitcast(FP8X4),
                rhs_scale=word_scales[:, cols],
                start=True,
                stop=True,
            )

        halves = [(slice(h * HALF, (h + 1) * HALF), slice(h * LIST_COLS // 2, (h + 1) * LIST_COLS // 2)) for h in range(2)]

        vs_win = sb.tile([P, TOKENS], U8, name="vs_win")
        ks_win = sb.tile([P, TOKENS], U8, name="ks_win")
        gf = sb.tile([P, TOKENS], F32, name="gf")
        nc.vector.memset(vs_win[:].bitcast(I32), 0)
        nc.vector.memset(ks_win[:].bitcast(I32), 0)
        nc.vector.memset(gf[:].bitcast(I32), 0)

        idx = lists.tile([P, LIST_COLS], U16, name="idx")
        idx4 = lists.tile([P, LIST_COLS], U16, name="idx4")
        pull_col = sb.tile([P, 1], F32, name="pull_col")
        nc.scalar.dma_start(out=pull_col[:], in_=pull)
        vs_rows = sb.tile([P, TOKENS], U8, name="vs_rows")
        load_scale_rows(vs_rows, vals_scales)
        nc.sync.dma_start(idx[:], offs)
        gout_raw = sb.tile([P, PACK, ROWS], F32, name="gout_raw")
        load_rows(gout_raw, gout)
        vw_win = sb.tile([P, TOKENS], U32, name="vw_win", tag="vw_then_base")
        load_words(vw_win, vals_words)
        query_raw = sb.tile([P, PACK, ROWS], F32, name="query_raw", tag="query_then_e1")
        load_rows(query_raw, query)
        nc.sync.dma_start(idx4[:], offs4)
        load_scale_rows(ks_win, keys_scales)

        g_codes, g_scales = quantise(gout_raw, "gout", "grouped_then_dquery", True)
        kw_win = sb.tile([P, TOKENS], U32, name="kw_win")
        load_words(kw_win, keys_words)
        dquery_raw = sb.tile([P, PACK, ROWS], F32, name="dquery_raw", tag="grouped_then_dquery", align_bytes=64)
        load_rows(dquery_raw, dquery)

        for quadrant in range(4):
            live = slice(32 * quadrant, 32 * quadrant + 4)
            nc.vector.tensor_copy(vs_win[live, :].bitcast(I32), vs_rows[live, :].bitcast(I32))
        vs = sb.tile([P, SLOTS], U8, name="vs", align_bytes=64)
        nc.vector.tensor_copy(vs[:], vs_win[:].indirect(idx[:]))

        q_codes, q_scales = quantise(query_raw, "query", "query_grouped", True)
        vw = sb.tile([P, SLOTS], U32, name="vw", align_bytes=64)
        c0 = psum.tile([P, SLOTS], F32, name="c0")
        e1 = sb.tile([P, SLOTS], F32, name="e1", tag="query_then_e1")
        s1 = sb.tile([P, SLOTS], F32, name="s1")
        for first, widths in ((0, (128,)), (128, (256, 128))):
            cols = slice(first, first + sum(widths))
            entries = slice(cols.start // 16, cols.stop // 16)
            nc.vector.tensor_copy(vw[:, cols], vw_win[:].indirect(idx[:, entries]))
            for width in widths:
                product(c0, slice(first, first + width), g_codes, g_scales, vw, vs)
                first += width
            nc.scalar.activation(e1[:, cols], c0[:, cols], ACT.Copy, scale=pull_col[:])
            nc.scalar.activation(s1[:].indirect(idx4[:, entries]), e1[:, cols], ACT.Copy)
        base_sb = sb.tile([P, TOKENS], F32, name="base_sb", tag="vw_then_base")
        nc.sync.dma_start(out=base_sb[:], in_=base)

        ks = sb.tile([P, SLOTS], U8, name="ks", align_bytes=64)
        nc.vector.tensor_copy(ks[:], ks_win[:].indirect(idx[:]))
        kw = sb.tile([P, SLOTS], U32, name="kw", align_bytes=64)
        a = psum.tile([P, SLOTS], F32, name="a")
        for first, widths in ((0, (256, 128)), (384, (128,))):
            cols = slice(first, first + sum(widths))
            entries = slice(cols.start // 16, cols.stop // 16)
            nc.vector.tensor_copy(kw[:, cols], kw_win[:].indirect(idx[:, entries]))
            for width in widths:
                product(a, slice(first, first + width), q_codes, q_scales, kw, ks)
                first += width
        dq_codes, dq_scales = quantise(dquery_raw, "dquery", "grouped_then_dr", False)
        ta = psum.tile([P, SLOTS], F32, name="ta")
        product(ta, slice(0, SLOTS), dq_codes, dq_scales, kw, ks)

        def column(name):
            return sb.tile([P, 1], F32, name=name)

        def wide(name):
            return sb.tile([P, SLOTS], F32, name=name)

        neg_max = sb.tile([P, 1], F32, name="neg_max", tag="grouped_then_dquery", align_bytes=64)
        nc.vector.tensor_reduce(out=neg_max[:], in_=a[:], axis=mybir.AxisListType.X, op=ALU.max, negate=True)
        p = wide("p")
        p_sum = column("p_sum")
        nc.scalar.activation(p[:], a[:], ACT.Exp, bias=neg_max[:], accum_out=p_sum[:])
        dr = sb.tile([P, SLOTS], F32, name="dr", tag="grouped_then_dr", align_bytes=64)
        nc.vector.tensor_tensor(dr[:], c0[:], s1[:], ALU.add)

        inv_sum = column("inv_sum")
        nc.vector.reciprocal(inv_sum[:], p_sum[:])
        neg_tp = wide("neg_tp")
        neg_tp_sum = column("neg_tp_sum")
        nc.vector.scalar_tensor_tensor(neg_tp[:], ta[:], -1.0, p[:], ALU.mult, ALU.mult, accum_out=neg_tp_sum[:])
        gain = column("gain")
        nc.vector.tensor_scalar(gain[:], inv_sum[:], inv_sum[:], 512.0, ALU.mult, ALU.mult)
        ta_dev = wide("ta_dev")
        nc.scalar.activation(ta_dev[:], ta[:], ACT.Identity, bias=neg_tp_sum[:], scale=p_sum[:])
        dr_terms = wide("dr_terms")
        dr_mean = column("dr_mean")
        nc.vector.scalar_tensor_tensor(dr_terms[:], dr[:], inv_sum[:], p[:], ALU.mult, ALU.mult, accum_out=dr_mean[:])
        tpdr_terms = wide("tpdr_terms")
        tpdr_sum = column("tpdr_sum")
        nc.vector.scalar_tensor_tensor(tpdr_terms[:], neg_tp[:], -1.0, dr[:], ALU.mult, ALU.mult, accum_out=tpdr_sum[:])
        cov = column("cov")
        cross = wide("cross")
        factor = wide("factor")
        for cols, entries in halves:
            nc.vector.scalar_tensor_tensor(cross[:, cols], dr[:, cols], dr_mean[:], ta_dev[:, cols], ALU.subtract, ALU.mult)
            if cols.start == 0:
                nc.vector.tensor_scalar(cov[:], dr_mean[:], neg_tp_sum[:], tpdr_sum[:], ALU.mult, ALU.add)
        for cols, entries in halves:
            nc.vector.tensor_scalar(factor[:, cols], cross[:, cols], cov[:], gain[:], ALU.subtract, ALU.mult)
        nc.vector.tensor_tensor(gf[:].indirect(idx[:]), factor[:], p[:], ALU.mult)

        start = 0
        for n, width in enumerate(STORE_WIDTHS):
            cols = slice(start, start + width)
            result = sb.tile([P, width], F32, name="result%d" % n)
            nc.vector.tensor_tensor(result[:], base_sb[:, cols], gf[:, cols], ALU.add)
            nc.sync.dma_start(out=out[:, cols], in_=result[:])
            start += width
